import numpy as np, ml_dtypes
CORES = [24,32,56,88,96,104,30,38,62,94,102,110]
N = 12
R, TK = 16, 256
def setup_inputs(rng):
    u = (rng.standard_normal((N, 128, R), dtype=np.float32) / 11).astype(ml_dtypes.bfloat16)
    return {"x": rng.standard_normal((N, 128, TK), dtype=np.float32).astype(ml_dtypes.bfloat16), "u": u, "ut": u.transpose(0, 2, 1).copy(), "vt": rng.standard_normal((N, R, 128), dtype=np.float32).astype(ml_dtypes.bfloat16)}
def setup_inputs_big(rng):
    d = setup_inputs(rng)
    for k in ("x", "u", "ut", "vt"): d[k] = (d[k].astype(np.float32) * 1024.0).astype(d[k].dtype)
    return d
def setup_inputs_small(rng):
    d = setup_inputs(rng)
    for k in ("x", "u", "ut", "vt"): d[k] = (d[k].astype(np.float32) * (1 / 1024.0)).astype(d[k].dtype)
    return d
def setup_inputs_apart(rng):
    d = setup_inputs(rng)
    f = (10.0 ** rng.permutation(np.linspace(-1.5, 1.5, N))).astype(np.float32).reshape(N, 1, 1)
    for k in ("x", "u", "ut", "vt"): d[k] = (d[k].astype(np.float32) * f).astype(d[k].dtype)
    return d
def tie_inputs(x):
    x = dict(x)
    x["ut"] = x["u"].transpose(0, 2, 1).copy()
    return x
def reference(x, u, ut, vt):
    X, U, VT = x.astype(np.float64), u.astype(np.float64), vt.astype(np.float64)
    y = np.stack([sum(VT[j].T @ (U[j].T @ X[r]) for j in range(N)) for r in range(N)])
    return {"y": y.astype(ml_dtypes.bfloat16 if x.dtype != np.float64 else np.float64)}

from concourse.bass import DstId, RemoteDMATransfer

N, RK, D, TK = 12, 16, 128, 256
WIDE = 4

SCRATCH = {
    "L": ("dram", [N, 128, 32], "bfloat16"),
    "W": ("sbuf", [128, 4 * D], "bfloat16"),
    "X": ("sbuf", [128, TK], "bfloat16"),
    "MT": ("sbuf", [128, D], "bfloat16"),
    "Y": ("sbuf", [128, TK], "bfloat16"),
    "PM": ("psum", [128, 512], "float32"),
    "PY": ("psum", [128, 512], "float32"),
}
SEMAPHORES = ["ld", "xl", "arrA", "arrB", "fwd", "sent", "la", "lb", "mm", "cm", "my", "cy", "st"]


def _plan(cores, topo):
    blocked = {s: [d for d in cores if d != s and not topo.may_write(s, d)] for s in cores}
    order = [s for s in cores if not blocked[s]] + [s for s in cores if blocked[s]]
    slot = {s: i for i, s in enumerate(order)}
    n_a = len([s for s in cores if not blocked[s]])

    def engines(src):
        m = -1
        for d in cores:
            if d != src:
                m &= topo.mask(src, d)
        bits = [1 << i for i in range(m.bit_length()) if (m >> i) & 1]
        return bits[::len(bits) // WIDE][:WIDE]

    def turn(src, dsts):
        i = cores.index(src)
        return sorted(dsts, key=lambda d: (cores.index(d) - i) % len(cores))

    def deal(src, dsts, n, sl, sem):
        e = engines(src)
        dsts = turn(src, dsts)
        return [(sl, dsts[i::n], e[i], 1, sem) for i in range(n)]

    calls = {s: [] for s in cores}
    relayed = {}
    for s in cores:
        if not blocked[s]:
            dsts = [d for d in cores if d != s]
            calls[s].append((False, deal(s, dsts, WIDE, slot[s], "arrA")))
    for s in cores:
        if blocked[s]:
            relay = [c for c in cores if c != s and topo.chip(c) == topo.chip(s)
                     and all(topo.may_write(c, d) for d in blocked[s])][0]
            relayed[relay] = s
            calls[s].append((False, [(slot[s], [relay], engines(s)[0], 1, "fwd")]))
            rest = [d for d in cores if d != s and d != relay and d not in blocked[s]]
            calls[s].append((False, deal(s, rest, min(WIDE, (len(rest) + 1) // 2), slot[s], "arrB")))
            calls[relay].append((True, deal(relay, blocked[s], min(WIDE, len(blocked[s])), slot[s], "arrB")))
    return calls, slot, n_a


def rank_program(g, core, T, topo):
    if T.rank_of(core) is None:
        return
    cores = list(T.cores)
    calls, slot, n_a = _plan(cores, topo)
    sem = T.sem
    expect = {"arrA": 0, "arrB": 0, "fwd": 0}
    for s in cores:
        for _, transfers in calls[s]:
            for _, dsts, _, n, name in transfers:
                if core in dsts:
                    expect[name] += n
    me = slot[core]
    ka, kb = RK * n_a, RK * (N - n_a)

    halves = ((g.sync, T.ut, 0), (g.scalar, T.vt, 1))
    for q, src, h in halves:
        q.dma_start(T.L[me, 64 * h:64 * h + 64, :], src[:, :]).then_inc(sem.ld, 16)
    g.sync.dma_start(T.X[:, :], T.x[:, :]).then_inc(sem.xl, 16)
    for q, src, h in halves:
        q.wait_ge(sem.ld, 32)
        if expect["arrA"]:
            q.wait_ge(sem.arrA, expect["arrA"])
        q.dma_start(T.W[0:ka, D * h:D * h + D], T.L[0:n_a, 64 * h:64 * h + 64, :]).then_inc(sem.la, 16)
        if expect["fwd"]:
            q.wait_ge(sem.fwd, expect["fwd"])
        if expect["arrB"]:
            q.wait_ge(sem.arrB, expect["arrB"])
        q.dma_start(T.W[0:kb, D * (2 + h):D * (3 + h)], T.L[n_a:N, 64 * h:64 * h + 64, :]).then_inc(sem.lb, 16)

    g.wait_ge(sem.ld, 32)
    sent = 0
    for relay_piece, transfers in calls[core]:
        if relay_piece:
            g.wait_ge(sem.fwd, expect["fwd"])
        ts = []
        for sl, dsts, mask, n, name in transfers:
            ids = []
            for d in dsts:
                rid, pid, _ = topo.addr(d)
                ids.append(DstId(rid=rid, pnc=pid))
            ts.append(RemoteDMATransfer(dst_ids=ids, dma_engine_mask=mask, remote_sem=sem[name],
                                        srcs=[T.L[sl]], dsts=[T.L[sl] for _ in dsts], alu_op=0))
            sent += n
        g.remote_dma_fused(ts, local_sem=sem.sent)
    g.wait_ge(sem.sent, sent)

    te, ve = g.tensor, g.vector
    te.wait_ge(sem.la, 32)
    te.matmul(T.PM[:, 0:D], T.W[0:ka, 0:D], T.W[0:ka, D:2 * D], start=True, stop=False)
    te.wait_ge(sem.lb, 32)
    te.matmul(T.PM[:, 0:D], T.W[0:kb, 2 * D:3 * D], T.W[0:kb, 3 * D:4 * D], start=False, stop=True).then_inc(sem.mm, 1)
    ve.wait_ge(sem.mm, 1)
    ve.tensor_copy(T.MT[:, :], T.PM[:, 0:D]).then_inc(sem.cm, 1)
    te.wait_ge(sem.xl, 16)
    te.wait_ge(sem.cm, 1)
    te.matmul(T.PY[:, 0:TK], T.MT[:, :], T.X[:, :], start=True, stop=True).then_inc(sem.my, 1)
    ve.wait_ge(sem.my, 1)
    ve.tensor_copy(T.Y[:, :], T.PY[:, 0:TK]).then_inc(sem.cy, 1)
    g.sync.wait_ge(sem.cy, 1)
    g.sync.dma_start(T.y[:, :], T.Y[:, :]).then_inc(sem.st, 16)
    g.sync.wait_ge(sem.st, 16)
